import numpy as np
CORES = [2,6,10,14,18,22,26,30]
N = 8
T, K = 16, 2
ROUTE = [[[0,4],[2,7],[5,1],[7,0],[6,5],[6,2],[0,1],[1,6],[2,1],[2,7],[2,6],[4,2],[6,1],[0,2],[0,2],[4,1]],[[1,0],[1,7],[5,7],[2,1],[5,0],[4,5],[2,1],[1,4],[7,5],[6,0],[7,6],[1,5],[2,1],[2,4],[1,6],[7,0]],[[2,0],[1,2],[0,5],[1,7],[4,7],[5,6],[1,0],[1,3],[6,3],[6,4],[6,5],[6,5],[0,2],[2,3],[0,3],[4,3]],[[5,3],[3,6],[6,3],[0,7],[0,1],[0,1],[5,4],[3,2],[7,6],[2,3],[0,1],[3,1],[6,3],[6,1],[0,2],[6,1]],[[5,4],[2,3],[3,0],[1,4],[7,4],[1,7],[5,2],[5,3],[0,3],[7,2],[4,7],[4,7],[7,4],[7,6],[6,1],[3,2]],[[0,1],[1,3],[3,0],[4,2],[7,6],[4,1],[5,7],[7,4],[7,2],[1,5],[5,1],[6,7],[5,4],[3,7],[2,5],[4,6]],[[3,4],[0,2],[4,2],[2,3],[2,3],[4,7],[6,2],[4,1],[5,2],[1,6],[4,1],[2,6],[0,6],[7,1],[0,7],[7,1]],[[4,1],[3,7],[1,6],[7,2],[2,5],[0,1],[4,5],[0,1],[5,2],[0,5],[3,5],[1,6],[7,0],[0,1],[3,1],[3,0]]]
ZW = 44
def setup_inputs(rng):
    return {"z": rng.standard_normal((N, 128, ZW), dtype=np.float32), "g": rng.random((N, 128, T * K), dtype=np.float32)}
def reference(z, g):
    y = np.zeros((N, 128, T), np.float64)
    fill = [0] * N
    for r in range(N):
        for t in range(T):
            for k, e in enumerate(ROUTE[r][t]):
                y[r][:, t] += g[r][:, t * K + k].astype(np.float64) * z[e][:, fill[e]].astype(np.float64)
                fill[e] += 1
    return {"y": y.astype(z.dtype)}

@@ -1,0 +1,145 @@
+from concourse.bass import DstId, RemoteDMATransfer
+from concourse.mybir import AluOpType
+
+W = 8
+FUSED = False
+PAIRS = False
+
+SCRATCH = {
+    "zs": ("sbuf", [128, 44], "float32"),
+    "gs": ("sbuf", [128, 32], "float32"),
+    "land": ("sbuf", [128, 8 * W], "float32"),
+    "pr": ("sbuf", [128, 32], "float32"),
+    "ys": ("sbuf", [128, 16], "float32"),
+}
+SEMAPHORES = ["zl", "gl", "sent", "a1", "a2", "a3", "a4", "vd", "yd", "st"]
+
+
+def way(topo, a, b):
+    ca, cb = topo.chip(a), topo.chip(b)
+    if a == b:
+        return 0
+    if ca == cb:
+        return 1
+    if topo.mates(ca, cb):
+        return 2
+    if topo.same_plane(ca, cb):
+        return 3
+    return 4
+
+
+def cover(el):
+    n = len(el)
+    if n == 0:
+        return []
+    idx = {x: i for i, x in enumerate(el)}
+    cands = []
+    for i in range(n):
+        cands.append((1 << i, (el[i], (1, 1), 1)))
+        for j in range(n):
+            dq, dp = el[j][0] - el[i][0], el[j][1] - el[i][1]
+            if dq > 0 and dp > 0:
+                m, cur, ln = 1 << i, el[i], 1
+                while (cur[0] + dq, cur[1] + dp) in idx:
+                    cur = (cur[0] + dq, cur[1] + dp)
+                    m |= 1 << idx[cur]
+                    ln += 1
+                    cands.append((m, (el[i], (dq, dp), ln)))
+    full = (1 << n) - 1
+    best = [99] * (full + 1)
+    how = [None] * (full + 1)
+    best[0] = 0
+    for s in range(full):
+        if best[s] == 99:
+            continue
+        low = 0
+        while (s >> low) & 1:
+            low += 1
+        for m, c in cands:
+            if (m >> low) & 1 and not (m & s) and best[s] + 1 < best[s | m]:
+                best[s | m] = best[s] + 1
+                how[s | m] = (s, c)
+    out, s = [], full
+    while s:
+        s, c = how[s]
+        out.append(c)
+    return out
+
+
+def run(buf, start, step, n):
+    return buf[:, start:start + (n - 1) * step + 1:step]
+
+
+def engines(w):
+    return 8 if w >= 2 else 16
+
+
+def rank_program(g, core, T, topo):
+    me = T.rank_of(core)
+    if me is None:
+        return
+    route, K, ZW = T.tables["ROUTE"], T.tables["K"], T.tables["ZW"]
+    N, NT = len(route), T.tables["T"]
+    cores = T.cores
+    fill = [0] * N
+    where = [[[] for e in range(N)] for r in range(N)]
+    for r in range(N):
+        for t in range(NT):
+            for k, e in enumerate(route[r][t]):
+                where[r][e].append((t * K + k, fill[e]))
+                fill[e] += 1
+
+    def slot(r, e):
+        order = sorted((x for x in range(N) if x != r), key=lambda x: (way(topo, cores[r], cores[x]), x))
+        return order.index(e)
+
+    arr = [None, T.sem.a1, T.sem.a2, T.sem.a3, T.sem.a4]
+
+    g.sync.dma_start(T.zs[:, :], T.z[:, :]).then_inc(T.sem.zl, 16)
+    g.sync.dma_start(T.gs[:, :], T.g[:, :]).then_inc(T.sem.gl, 16)
+
+    g.wait_ge(T.sem.zl, 16)
+    sent = 0
+    for r in range(N):
+        blk = where[r][me]
+        if r == me or not blk:
+            continue
+        w = way(topo, core, cores[r])
+        rid, pid, se = topo.addr(cores[r])
+        ne = engines(w)
+        o, n = blk[0][1], len(blk)
+        s = slot(r, me) * W
+        g.remote_dma(T.land[:, s:s + n], T.zs[:, o:o + n], arr[w], T.sem.sent, pid, rid, (1 << ne) - 1)
+        sent += ne
+
+    v = g.vector
+    v.wait_ge(T.sem.gl, 16)
+    v.wait_ge(T.sem.zl, 16)
+    nops = 0
+    for w in range(5):
+        el, expect = [], 0
+        for e in range(N):
+            blk = where[me][e]
+            if way(topo, core, cores[e]) != w or not blk:
+                continue
+            if w == 0:
+                el += blk
+            else:
+                expect += engines(w)
+                base = slot(me, e) * W - blk[0][1]
+                el += [(q, base + c) for q, c in blk]
+        if expect:
+            v.wait_ge(arr[w], expect)
+        src = T.zs if w == 0 else T.land
+        ops = cover(el) if PAIRS else [(x, (1, 1), 1) for x in el]
+        for (q, p), (dq, dp), n in ops:
+            v.tensor_tensor(run(T.pr, q, dq, n), run(src, p, dp, n), run(T.gs, q, dq, n),
+                            AluOpType.mult).then_inc(T.sem.vd, 1)
+            nops += 1
+    v.wait_ge(T.sem.vd, nops)
+    v.tensor_tensor(T.ys[:, :], run(T.pr, 0, K, NT), run(T.pr, 1, K, NT), AluOpType.add).then_inc(T.sem.yd, 1)
+
+    g.sync.wait_ge(T.sem.yd, 1)
+    g.sync.dma_start(T.y[:, :], T.ys[:, :]).then_inc(T.sem.st, 16)
+    g.sync.wait_ge(T.sem.st, 16)
+    g.wait_ge(T.sem.sent, sent)

@@ -1,14 +1,13 @@
 from concourse.bass import DstId, RemoteDMATransfer
 from concourse.mybir import AluOpType
 
-W = 8
-FUSED = False
-PAIRS = False
+MODE = "sep"
+ORDER = [0, 4, 3, 2, 1]
 
 SCRATCH = {
     "zs": ("sbuf", [128, 44], "float32"),
     "gs": ("sbuf", [128, 32], "float32"),
-    "land": ("sbuf", [128, 8 * W], "float32"),
+    "land": ("sbuf", [128, 320], "float32"),
     "pr": ("sbuf", [128, 32], "float32"),
     "ys": ("sbuf", [128, 16], "float32"),
 }
@@ -70,10 +69,6 @@ def run(buf, start, step, n):
     return buf[:, start:start + (n - 1) * step + 1:step]
 
 
-def engines(w):
-    return 8 if w >= 2 else 16
-
-
 def rank_program(g, core, T, topo):
     me = T.rank_of(core)
     if me is None:
@@ -89,9 +84,35 @@ def rank_program(g, core, T, topo):
                 where[r][e].append((t * K + k, fill[e]))
                 fill[e] += 1
 
-    def slot(r, e):
-        order = sorted((x for x in range(N) if x != r), key=lambda x: (way(topo, cores[r], cores[x]), x))
-        return order.index(e)
+    def wy(a, b):
+        return way(topo, cores[a], cores[b])
+
+    def peers(e):
+        return sorted((x for x in range(N) if x != e), key=lambda x: (ORDER.index(wy(e, x)), x))
+
+    def plan(e):
+        ds = [r for r in peers(e) if where[r][e]]
+        if MODE == "sep":
+            return [[(0, 16 if wy(e, r) == 1 else 8, [r], where[r][e][0][1], len(where[r][e]))] for r in ds]
+        if MODE == "multi":
+            return [[(0, 8, [r for r in ds if wy(e, r) != 1], 0, ZW), (8, 8, [r for r in ds if wy(e, r) == 1], 0, ZW)]]
+        return []
+
+    def found(r, e):
+        for call in plan(e):
+            for first, ne, ds, o, wd in call:
+                if r in ds:
+                    return ne, o, wd
+        return None
+
+    def base(r, e):
+        b = 0
+        for x in peers(r):
+            if x == e:
+                return b
+            if where[r][x]:
+                b += found(r, x)[2]
+        return None
 
     arr = [None, T.sem.a1, T.sem.a2, T.sem.a3, T.sem.a4]
 
@@ -100,39 +121,45 @@ def rank_program(g, core, T, topo):
 
     g.wait_ge(T.sem.zl, 16)
     sent = 0
-    for r in range(N):
-        blk = where[r][me]
-        if r == me or not blk:
-            continue
-        w = way(topo, core, cores[r])
-        rid, pid, se = topo.addr(cores[r])
-        ne = engines(w)
-        o, n = blk[0][1], len(blk)
-        s = slot(r, me) * W
-        g.remote_dma(T.land[:, s:s + n], T.zs[:, o:o + n], arr[w], T.sem.sent, pid, rid, (1 << ne) - 1)
-        sent += ne
+    for call in plan(me):
+        trs = []
+        for first, ne, ds, o, wd in call:
+            ids, dsts = [], []
+            for r in ds:
+                rid, pid, se = topo.addr(cores[r])
+                b = base(r, me)
+                ids.append(DstId(rid=rid, pnc=pid))
+                dsts.append(T.land[:, b:b + wd])
+            trs.append((ids, dsts, ((1 << ne) - 1) << first, arr[wy(me, ds[0])], T.zs[:, o:o + wd]))
+            sent += ne
+        if len(trs) == 1 and len(trs[0][0]) == 1:
+            ids, dsts, mask, sem, src = trs[0]
+            g.remote_dma(dsts[0], src, sem, T.sem.sent, ids[0].pnc, ids[0].rid, mask)
+        else:
+            g.remote_dma_fused([RemoteDMATransfer(dst_ids=ids, dma_engine_mask=mask, remote_sem=sem, srcs=[src],
+                                                  dsts=dsts) for ids, dsts, mask, sem, src in trs],
+                               local_sem=T.sem.sent)
 
     v = g.vector
     v.wait_ge(T.sem.gl, 16)
     v.wait_ge(T.sem.zl, 16)
     nops = 0
-    for w in range(5):
+    for w in ORDER:
         el, expect = [], 0
         for e in range(N):
             blk = where[me][e]
-            if way(topo, core, cores[e]) != w or not blk:
+            if wy(me, e) != w or not blk:
                 continue
             if w == 0:
                 el += blk
             else:
-                expect += engines(w)
-                base = slot(me, e) * W - blk[0][1]
-                el += [(q, base + c) for q, c in blk]
+                ne, o, wd = found(me, e)
+                expect += ne
+                el += [(q, base(me, e) - o + c) for q, c in blk]
         if expect:
             v.wait_ge(arr[w], expect)
         src = T.zs if w == 0 else T.land
-        ops = cover(el) if PAIRS else [(x, (1, 1), 1) for x in el]
-        for (q, p), (dq, dp), n in ops:
+        for (q, p), (dq, dp), n in cover(el):
             v.tensor_tensor(run(T.pr, q, dq, n), run(src, p, dp, n), run(T.gs, q, dq, n),
                             AluOpType.mult).then_inc(T.sem.vd, 1)
             nops += 1

@@ -1,13 +1,12 @@
 from concourse.bass import DstId, RemoteDMATransfer
 from concourse.mybir import AluOpType
 
-MODE = "sep"
-ORDER = [0, 4, 3, 2, 1]
+ORDER = [0, 1, 4, 3, 2]
 
 SCRATCH = {
     "zs": ("sbuf", [128, 44], "float32"),
     "gs": ("sbuf", [128, 32], "float32"),
-    "land": ("sbuf", [128, 320], "float32"),
+    "land": ("sbuf", [128, 64], "float32"),
     "pr": ("sbuf", [128, 32], "float32"),
     "ys": ("sbuf", [128, 16], "float32"),
 }
@@ -91,17 +90,23 @@ def rank_program(g, core, T, topo):
         return sorted((x for x in range(N) if x != e), key=lambda x: (ORDER.index(wy(e, x)), x))
 
     def plan(e):
-        ds = [r for r in peers(e) if where[r][e]]
-        if MODE == "sep":
-            return [[(0, 16 if wy(e, r) == 1 else 8, [r], where[r][e][0][1], len(where[r][e]))] for r in ds]
-        if MODE == "multi":
-            return [[(0, 8, [r for r in ds if wy(e, r) != 1], 0, ZW), (8, 8, [r for r in ds if wy(e, r) == 1], 0, ZW)]]
-        return []
+        calls = []
+        for w in ORDER:
+            rs = [r for r in range(N) if w >= 2 and wy(e, r) == w and where[r][e]]
+            if rs:
+                ne = 8 // len(rs)
+                calls.append([(i * ne, ne, r) for i, r in enumerate(rs)])
+        calls[0] += [(8, 8, r) for r in range(N) if wy(e, r) == 1 and where[r][e]]
+        out = []
+        for call in calls:
+            wd = max(len(where[r][e]) for first, ne, r in call)
+            out.append([(first, ne, r, min(where[r][e][0][1], ZW - wd), wd) for first, ne, r in call])
+        return out
 
     def found(r, e):
         for call in plan(e):
-            for first, ne, ds, o, wd in call:
-                if r in ds:
+            for first, ne, x, o, wd in call:
+                if x == r:
                     return ne, o, wd
         return None
 
@@ -123,22 +128,13 @@ def rank_program(g, core, T, topo):
     sent = 0
     for call in plan(me):
         trs = []
-        for first, ne, ds, o, wd in call:
-            ids, dsts = [], []
-            for r in ds:
-                rid, pid, se = topo.addr(cores[r])
-                b = base(r, me)
-                ids.append(DstId(rid=rid, pnc=pid))
-                dsts.append(T.land[:, b:b + wd])
-            trs.append((ids, dsts, ((1 << ne) - 1) << first, arr[wy(me, ds[0])], T.zs[:, o:o + wd]))
+        for first, ne, r, o, wd in call:
+            rid, pid, se = topo.addr(cores[r])
+            b = base(r, me)
+            trs.append(RemoteDMATransfer(dst_ids=[DstId(rid=rid, pnc=pid)], dma_engine_mask=((1 << ne) - 1) << first,
+                                         remote_sem=arr[wy(me, r)], src=T.zs[:, o:o + wd], dst=T.land[:, b:b + wd]))
             sent += ne
-        if len(trs) == 1 and len(trs[0][0]) == 1:
-            ids, dsts, mask, sem, src = trs[0]
-            g.remote_dma(dsts[0], src, sem, T.sem.sent, ids[0].pnc, ids[0].rid, mask)
-        else:
-            g.remote_dma_fused([RemoteDMATransfer(dst_ids=ids, dma_engine_mask=mask, remote_sem=sem, srcs=[src],
-                                                  dsts=dsts) for ids, dsts, mask, sem, src in trs],
-                               local_sem=T.sem.sent)
+        g.remote_dma_fused(trs, local_sem=T.sem.sent)
 
     v = g.vector
     v.wait_ge(T.sem.gl, 16)

@@ -72,7 +72,7 @@ def rank_program(g, core, T, topo):
     me = T.rank_of(core)
     if me is None:
         return
-    route, K, ZW = T.tables["ROUTE"], T.tables["K"], T.tables["ZW"]
+    route, K = T.tables["ROUTE"], T.tables["K"]
     N, NT = len(route), T.tables["T"]
     cores = T.cores
     fill = [0] * N
@@ -100,7 +100,7 @@ def rank_program(g, core, T, topo):
         out = []
         for call in calls:
             wd = max(len(where[r][e]) for first, ne, r in call)
-            out.append([(first, ne, r, min(where[r][e][0][1], ZW - wd), wd) for first, ne, r in call])
+            out.append([(first, ne, r, min(where[r][e][0][1], fill[e] - wd), wd) for first, ne, r in call])
         return out
 
     def found(r, e):
@@ -121,7 +121,7 @@ def rank_program(g, core, T, topo):
 
     arr = [None, T.sem.a1, T.sem.a2, T.sem.a3, T.sem.a4]
 
-    g.sync.dma_start(T.zs[:, :], T.z[:, :]).then_inc(T.sem.zl, 16)
+    g.sync.dma_start(T.zs[:, 0:fill[me]], T.z[:, 0:fill[me]]).then_inc(T.sem.zl, 16)
     g.sync.dma_start(T.gs[:, :], T.g[:, :]).then_inc(T.sem.gl, 16)
 
     g.wait_ge(T.sem.zl, 16)

from concourse.bass import DstId, RemoteDMATransfer
from concourse.mybir import AluOpType

ORDER = [0, 1, 4, 3, 2]

SCRATCH = {
    "zs": ("sbuf", [128, 44], "float32"),
    "gs": ("sbuf", [128, 32], "float32"),
    "land": ("sbuf", [128, 64], "float32"),
    "pr": ("sbuf", [128, 32], "float32"),
    "ys": ("sbuf", [128, 16], "float32"),
}
SEMAPHORES = ["zl", "gl", "sent", "a1", "a2", "a3", "a4", "vd", "yd", "st"]


def way(topo, a, b):
    ca, cb = topo.chip(a), topo.chip(b)
    if a == b:
        return 0
    if ca == cb:
        return 1
    if topo.mates(ca, cb):
        return 2
    if topo.same_plane(ca, cb):
        return 3
    return 4


def cover(el):
    n = len(el)
    if n == 0:
        return []
    idx = {x: i for i, x in enumerate(el)}
    cands = []
    for i in range(n):
        cands.append((1 << i, (el[i], (1, 1), 1)))
        for j in range(n):
            dq, dp = el[j][0] - el[i][0], el[j][1] - el[i][1]
            if dq > 0 and dp > 0:
                m, cur, ln = 1 << i, el[i], 1
                while (cur[0] + dq, cur[1] + dp) in idx:
                    cur = (cur[0] + dq, cur[1] + dp)
                    m |= 1 << idx[cur]
                    ln += 1
                    cands.append((m, (el[i], (dq, dp), ln)))
    full = (1 << n) - 1
    best = [99] * (full + 1)
    how = [None] * (full + 1)
    best[0] = 0
    for s in range(full):
        if best[s] == 99:
            continue
        low = 0
        while (s >> low) & 1:
            low += 1
        for m, c in cands:
            if (m >> low) & 1 and not (m & s) and best[s] + 1 < best[s | m]:
                best[s | m] = best[s] + 1
                how[s | m] = (s, c)
    out, s = [], full
    while s:
        s, c = how[s]
        out.append(c)
    return out


def run(buf, start, step, n):
    return buf[:, start:start + (n - 1) * step + 1:step]


def rank_program(g, core, T, topo):
    me = T.rank_of(core)
    if me is None:
        return
    route, K = T.tables["ROUTE"], T.tables["K"]
    N, NT = len(route), T.tables["T"]
    cores = T.cores
    fill = [0] * N
    where = [[[] for e in range(N)] for r in range(N)]
    for r in range(N):
        for t in range(NT):
            for k, e in enumerate(route[r][t]):
                where[r][e].append((t * K + k, fill[e]))
                fill[e] += 1

    def wy(a, b):
        return way(topo, cores[a], cores[b])

    def peers(e):
        return sorted((x for x in range(N) if x != e), key=lambda x: (ORDER.index(wy(e, x)), x))

    def plan(e):
        calls = []
        for w in ORDER:
            rs = [r for r in range(N) if w >= 2 and wy(e, r) == w and where[r][e]]
            if rs:
                ne = 8 // len(rs)
                calls.append([(i * ne, ne, r) for i, r in enumerate(rs)])
        calls[0] += [(8, 8, r) for r in range(N) if wy(e, r) == 1 and where[r][e]]
        out = []
        for call in calls:
            wd = max(len(where[r][e]) for first, ne, r in call)
            out.append([(first, ne, r, min(where[r][e][0][1], fill[e] - wd), wd) for first, ne, r in call])
        return out

    def found(r, e):
        for call in plan(e):
            for first, ne, x, o, wd in call:
                if x == r:
                    return ne, o, wd
        return None

    def base(r, e):
        b = 0
        for x in peers(r):
            if x == e:
                return b
            if where[r][x]:
                b += found(r, x)[2]
        return None

    arr = [None, T.sem.a1, T.sem.a2, T.sem.a3, T.sem.a4]

    g.sync.dma_start(T.zs[:, 0:fill[me]], T.z[:, 0:fill[me]]).then_inc(T.sem.zl, 16)
    g.sync.dma_start(T.gs[:, :], T.g[:, :]).then_inc(T.sem.gl, 16)

    g.wait_ge(T.sem.zl, 16)
    sent = 0
    for call in plan(me):
        trs = []
        for first, ne, r, o, wd in call:
            rid, pid, se = topo.addr(cores[r])
            b = base(r, me)
            trs.append(RemoteDMATransfer(dst_ids=[DstId(rid=rid, pnc=pid)], dma_engine_mask=((1 << ne) - 1) << first,
                                         remote_sem=arr[wy(me, r)], src=T.zs[:, o:o + wd], dst=T.land[:, b:b + wd]))
            sent += ne
        g.remote_dma_fused(trs, local_sem=T.sem.sent)

    v = g.vector
    v.wait_ge(T.sem.gl, 16)
    v.wait_ge(T.sem.zl, 16)
    nops = 0
    for w in ORDER:
        el, expect = [], 0
        for e in range(N):
            blk = where[me][e]
            if wy(me, e) != w or not blk:
                continue
            if w == 0:
                el += blk
            else:
                ne, o, wd = found(me, e)
                expect += ne
                el += [(q, base(me, e) - o + c) for q, c in blk]
        if expect:
            v.wait_ge(arr[w], expect)
        src = T.zs if w == 0 else T.land
        for (q, p), (dq, dp), n in cover(el):
            v.tensor_tensor(run(T.pr, q, dq, n), run(src, p, dp, n), run(T.gs, q, dq, n),
                            AluOpType.mult).then_inc(T.sem.vd, 1)
            nops += 1
    v.wait_ge(T.sem.vd, nops)
    v.tensor_tensor(T.ys[:, :], run(T.pr, 0, K, NT), run(T.pr, 1, K, NT), AluOpType.add).then_inc(T.sem.yd, 1)

    g.sync.wait_ge(T.sem.yd, 1)
    g.sync.dma_start(T.y[:, :], T.ys[:, :]).then_inc(T.sem.st, 16)
    g.sync.wait_ge(T.sem.st, 16)
    g.wait_ge(T.sem.sent, sent)
